import numpy as np
import ml_dtypes


def mxq(x, axis, fmt="e4m3"):
    dtype, down = {"e4m3": (ml_dtypes.float8_e4m3fn, 7), "e5m2": (ml_dtypes.float8_e5m2, 14)}[fmt]
    v = np.moveaxis(np.asarray(x, np.float32).astype(ml_dtypes.bfloat16).astype(np.float64), axis, -1)
    blocks = v.reshape(v.shape[:-1] + (-1, 32))
    amax = np.abs(blocks).max(-1, keepdims=True)
    byte = np.maximum(np.where(amax > 0, np.frexp(amax)[1] - 1 + 127, 0) - down, 1)
    scale = np.exp2(byte - 127.0)
    codes = (blocks / scale).astype(np.float32).astype(dtype).astype(np.float64)
    return np.moveaxis((codes * scale).reshape(v.shape), -1, axis)


WIDE = False


def mx_kscale(k):
    if not WIDE:
        return np.ones(k)
    levels = np.array([10, -10, 5, -5, 0])
    if k % 512:
        return np.exp2(np.random.permutation(np.resize(levels, k // 32))).repeat(32)
    a = np.empty((k // 512, 16))
    for p in range(k // 512):
        a[p, :8] = np.random.permutation(np.resize(levels, 8))
        for g in range(8):
            far = levels[np.abs(levels - a[p, g]) >= 10]
            a[p, g + 8] = far[np.random.randint(len(far))]
    return np.exp2(a.ravel()).repeat(32)


def f64(x):
    return np.asarray(x).astype(np.float64)


def striped(idx):
    return np.tile(np.asarray(idx).reshape(-1, 16).T, (8, 1)).astype(np.uint16)


def unstriped(offs):
    return offs[:16].T.reshape(-1).astype(np.int64)


E2M1 = np.array([0.0, 0.5, 1.0, 1.5, 2.0, 3.0, 4.0, 6.0, -0.0, -0.5, -1.0, -1.5, -2.0, -3.0, -4.0, -6.0])


def pack_weight(w, fmt):
    k, n = w.shape
    w = f64(np.asarray(w, np.float32).astype(ml_dtypes.bfloat16)).reshape(k // 32, 32, n)
    amax = np.abs(w).max(1)
    if fmt == "e4m3":
        byte = np.frexp(amax)[1] - 1 + 127 - 7
    else:
        mant, ex = np.frexp(amax / 6.0)
        byte = np.where(mant > 0.5, ex, ex - 1) + 127
    byte = np.clip(np.where(amax > 0, byte, 1), 1, 254)
    scaled = (w * np.exp2(127.0 - byte)[:, None, :]).reshape(k, n).astype(np.float32)
    by_word = np.ascontiguousarray(scaled.reshape(k // 512, 128, 4, n).transpose(0, 1, 3, 2))
    if fmt == "e4m3":
        words = by_word.astype(ml_dtypes.float8_e4m3fn).view(np.uint8)
    else:
        c = by_word.astype(ml_dtypes.float4_e2m1fn).view(np.uint8) & 0xF
        words = (c[..., 0::2] | (c[..., 1::2] << 4)).reshape(k // 512, 128, 2 * n)
    return np.ascontiguousarray(words), np.ascontiguousarray(byte.astype(np.uint8).reshape(k // 512, 16, n))


def unpack_weight(words, scales, fmt):
    g, _, n = scales.shape
    words = np.ascontiguousarray(words).reshape(g, 128, n, -1)
    if fmt == "e4m3":
        vals = words.view(ml_dtypes.float8_e4m3fn).astype(np.float64)
    else:
        nib = np.empty((g, 128, n, 4), np.uint8)
        nib[..., 0::2] = words & 0xF
        nib[..., 1::2] = words >> 4
        vals = E2M1[nib]
    vals = vals * np.repeat(np.exp2(scales.astype(np.float64) - 127.0), 8, axis=1)[..., None]
    return vals.transpose(0, 1, 3, 2).reshape(g * 512, n)


D, E, T, I, Q = 512, 512, 2048, 512, 128


def setup_inputs():
    n = np.random.standard_normal
    idx2 = np.random.permutation(I)[:I]
    idx = np.random.permutation(T)[:I]
    fd = mx_kscale(D)
    fe = mx_kscale(E)
    keysp = pack_weight(n((D, T)) / fd[:, None], "e4m3")
    valsp = pack_weight(n((E, T)) / fe[:, None], "e4m3")
    return {
        "query": (n((D, Q)) * 0.8 / np.sqrt(D) * fd[:, None]).astype(np.float32),
        "keys_words": keysp[0],
        "keys_scales": keysp[1],
        "reserve": (np.random.uniform(0.5, 2.0, (Q, 1))).astype(np.float32),
        "gout": (n((E, Q)) * 1 / np.sqrt(E) * fe[:, None]).astype(np.float32),
        "vals_words": valsp[0],
        "vals_scales": valsp[1],
        "dquery": (n((D, Q)) * 1.0 / np.sqrt(D) * fd[:, None]).astype(np.float32),
        "base": (0.5 * n((Q, T))).astype(np.float32),
        "offs2": striped(idx2),
        "offs": striped(idx),
    }


def reference(query, keys_words, keys_scales, reserve, gout, vals_words, vals_scales, dquery, base, offs2, offs):
    idx2 = unstriped(offs2)
    idx = unstriped(offs)
    keysu = unpack_weight(keys_words, keys_scales, "e4m3")
    valsu = unpack_weight(vals_words, vals_scales, "e4m3")
    queryq = mxq(f64(query), 0, "e4m3")
    keysidxg = keysu[:, idx]
    a = queryq.T @ keysidxg
    dqueryq = mxq(f64(dquery), 0, "e4m3")
    ta = dqueryq.T @ keysidxg
    p = np.exp(a)
    z = np.sum(p, axis=1, keepdims=True)
    r = p / (p + p[:, idx2] + f64(reserve))
    goutq = mxq(f64(gout), 0, "e4m3")
    valsidxg = valsu[:, idx]
    c0 = goutq.T @ valsidxg
    dr = c0 * p / z
    dz = np.sum(c0 * r * p / np.square(z) * (-1.0), axis=1, keepdims=True)
    e1 = dr * p / np.square(p + p[:, idx2] + f64(reserve)) * (-1.0)
    s1 = np.zeros((Q, I))
    s1[:, idx2] = e1
    dp = c0 * r / z + dr / (p + p[:, idx2] + f64(reserve)) + dz + s1 - dr * p / np.square(p + p[:, idx2] + f64(reserve))
    tp = ta * p
    tz = np.sum(tp, axis=1, keepdims=True)
    tr = (tp - (tp + tp[:, idx2]) * p / (p + p[:, idx2] + f64(reserve))) / (p + p[:, idx2] + f64(reserve))
    tdr = (tp - tz * p / z) / z * c0
    tdz = np.sum((tr * c0 * p + tp * c0 * r - tz * z * 2.0 * c0 * r * p / np.square(z)) / np.square(z) * (-1.0), axis=1, keepdims=True)
    te1 = (tdr * p + tp * dr - (tp + tp[:, idx2]) * (p + p[:, idx2] + f64(reserve)) * 2.0 * dr * p / np.square(p + p[:, idx2] + f64(reserve))) / np.square(p + p[:, idx2] + f64(reserve)) * (-1.0)
    ts1 = np.zeros((Q, I))
    ts1[:, idx2] = te1
    tdp = (tr * c0 - tz * c0 * r / z) / z + (tdr - (tp + tp[:, idx2]) * dr / (p + p[:, idx2] + f64(reserve))) / (p + p[:, idx2] + f64(reserve)) + tdz + ts1 - (tdr * p + tp * dr - (tp + tp[:, idx2]) * (p + p[:, idx2] + f64(reserve)) * 2.0 * dr * p / np.square(p + p[:, idx2] + f64(reserve))) / np.square(p + p[:, idx2] + f64(reserve))
    tda = tdp * p + tp * dp
    gs = tda * 512.0
    gf = np.zeros((Q, T))
    gf[:, idx] = gs
    y = f64(base) + gf
    return y

@@ -1,0 +1,224 @@
+from contextlib import ExitStack
+
+import concourse.mybir as mybir
+from concourse.masks import make_identity
+
+F32 = mybir.dt.float32
+BF16 = mybir.dt.bfloat16
+I32 = mybir.dt.int32
+U32 = mybir.dt.uint32
+U16 = mybir.dt.uint16
+U8 = mybir.dt.uint8
+FP8X4 = mybir.dt.float8_e4m3fn_x4
+ACT = mybir.ActivationFunctionType
+ALU = mybir.AluOpType
+
+P = 128
+PACK = 4
+T = 2048
+I = 512
+Q = 128
+SPARE = 64
+GAIN = 512.0
+OUT_EDGES = (0, 640, 1280, 1792, 2048)
+FLOPS = 3 * 2 * 512 * Q * I
+
+
+def tile_attend_hvneighbourshare_s_kernel(tc, query, keys_words, keys_scales, reserve, gout, vals_words, vals_scales, dquery, base, offs2, offs, out):
+    nc = tc.nc
+    with ExitStack() as ctx:
+        sb = ctx.enter_context(tc.tile_pool(name="sb", bufs=1))
+        shared = ctx.enter_context(tc.tile_pool(name="shared", bufs=1))
+        ps = ctx.enter_context(tc.psum_pool(name="ps", bufs=1))
+
+        def wide(name, cols=I):
+            return sb.tile([P, cols], F32, name=name)
+
+        def column(name):
+            return sb.tile([P, 1], F32, name=name)
+
+        def load_scales(name, scales, clearer, tag):
+            plane = sb.tile([P, T], U8, name=name, tag=tag, align_bytes=64)
+            clearer.memset(plane[:].bitcast(I32), 0)
+            for quad in range(4):
+                nc.sync.dma_start(plane[32 * quad : 32 * quad + 4, :].bitcast(I32), scales[0][4 * quad : 4 * quad + 4, :].bitcast(I32))
+            return plane
+
+        def load_words(pool_words, words):
+            nc.sync.dma_start(pool_words[:], words[0].rearrange("p n t -> p (n t)").bitcast(I32))
+            return pool_words
+
+        def load_rows(name, rows, offset):
+            raw = shared.tile([P, PACK, Q], F32, name=name, offset=offset)
+            nc.sync.dma_start(raw[:], rows.rearrange("(p j) w -> p j w", j=PACK))
+            return raw
+
+        def quantise(name, grouped):
+            codes = sb.tile([P, Q], U32, name=name + "_codes", align_bytes=64)
+            scales = sb.tile([P, Q], U8, name=name + "_scales", align_bytes=64)
+            nc.vector.quantize_mx(out=codes[:].bitcast(FP8X4), scales=scales[:], in_=grouped[:].rearrange("p w j -> p (w j)"))
+            return codes, scales
+
+        def gather_words(name, pool_words):
+            picked = sb.tile([P, I], U32, name=name, align_bytes=64)
+            nc.vector.tensor_copy(picked[:], pool_words[:].bitcast(U32).indirect(tokens[:]))
+            return picked
+
+        def gather_scales(name, plane):
+            picked = sb.tile([P, I], U8, name=name, align_bytes=64)
+            nc.vector.tensor_copy(picked[:], plane[:].indirect(tokens[:]))
+            return picked
+
+        def product(name, rows, words, scales):
+            bank = ps.tile([P, I], F32, name=name)
+            nc.tensor.matmul_mx(out=bank[:], lhsT=rows[0][:].bitcast(FP8X4), lhsT_scale=rows[1][:], rhs=words[:].bitcast(FP8X4), rhs_scale=scales[:], start=True, stop=True)
+            return bank
+
+        tokens = sb.tile([P, I // 16], U16, name="tokens")
+        nc.sync.dma_start(tokens[:], offs)
+        q_raw = load_rows("q_raw", query, 4 * T)
+        links = sb.tile([P, I // 16], U16, name="links")
+        nc.sync.dma_start(links[:], offs2)
+        k_plane = load_scales("k_plane", keys_scales, nc.vector, "k_plane")
+        ident = wide("ident", P)
+        make_identity(nc, ident[:])
+        k_pool = load_words(shared.tile([P, T], I32, name="k_pool", offset=0), keys_words)
+
+        p_win = wide("p_win", I + SPARE)
+        tp_win = wide("tp_win", I + SPARE)
+        nc.gpsimd.memset(p_win[:, I:], 0.0)
+        nc.gpsimd.memset(tp_win[:, I:], 0.0)
+        placed = wide("placed", T)
+        nc.gpsimd.memset(placed[:], 0.0)
+        p = p_win[:, :I]
+        tp = tp_win[:, :I]
+
+        q_grouped = sb.tile([P, Q, PACK], BF16, name="q_grouped", tag="q_grouped", align_bytes=64)
+        nc.vector.tensor_copy(q_grouped[:], q_raw[:].rearrange("p j w -> p w j"))
+        dq_raw = load_rows("dq_raw", dquery, 4 * T + 32)
+        rho = shared.tile([P, 1], F32, name="rho", offset=4 * T)
+        nc.sync.dma_start(rho[:], reserve)
+        k_scales = gather_scales("k_scales", k_plane)
+        q_mx = quantise("q", q_grouped)
+        v_plane = load_scales("v_plane", vals_scales, nc.gpsimd, "q_grouped")
+        k_words = gather_words("k_words", k_pool)
+        v_pool = load_words(shared.tile([P, T], I32, name="v_pool", offset=0), vals_words)
+        a = product("a", q_mx, k_words, k_scales)
+
+        dq_grouped = sb.tile([P, Q, PACK], BF16, name="dq_grouped", align_bytes=64)
+        nc.scalar.copy(dq_grouped[:], dq_raw[:].rearrange("p j w -> p w j"))
+        g_raw = load_rows("g_raw", gout, 4 * T + 32)
+        dq_mx = quantise("dq", dq_grouped)
+        x = product("x", dq_mx, k_words, k_scales)
+        v_scales = gather_scales("v_scales", v_plane)
+
+        z = column("z")
+        nc.scalar.activation(p, a[:], ACT.Exp, accum_out=z[:])
+        p_rho = wide("p_rho")
+        nc.scalar.activation(p_rho[:], p, ACT.Identity, bias=rho[:])
+        z_rsqrt = column("z_rsqrt")
+        nc.scalar.activation(z_rsqrt[:], z[:], ACT.Abs_reciprocal_sqrt)
+        z_inv = column("z_inv")
+        nc.scalar.activation(z_inv[:], z_rsqrt[:], ACT.Square)
+
+        tz = column("tz")
+        nc.vector.scalar_tensor_tensor(tp, x[:], 1.0, p, ALU.mult, ALU.mult, accum_out=tz[:])
+        den = wide("den")
+        nc.vector.tensor_tensor(den[:], p_win[:].indirect(links[:]), p_rho[:], ALU.add)
+
+        tp_copy = wide("tp_copy")
+        nc.scalar.copy(tp_copy[:], tp)
+        den_rsqrt = wide("den_rsqrt")
+        nc.scalar.activation(den_rsqrt[:], den[:], ACT.Abs_reciprocal_sqrt)
+        u = wide("u")
+        nc.scalar.activation(u[:], den_rsqrt[:], ACT.Square)
+
+        t_den = wide("t_den")
+        nc.vector.tensor_tensor(t_den[:], tp_win[:].indirect(links[:]), tp_copy[:], ALU.add)
+
+        g_grouped = sb.tile([P, Q, PACK], BF16, name="g_grouped", align_bytes=64)
+        nc.scalar.copy(g_grouped[:], g_raw[:].rearrange("p j w -> p w j"))
+        v_words = gather_words("v_words", v_pool)
+        base_sb = shared.tile([P, T], F32, name="base_sb", offset=0)
+        nc.sync.dma_start(base_sb[:], base)
+        g_mx = quantise("g", g_grouped)
+        c = product("c", g_mx, v_words, v_scales)
+
+        tau = column("tau")
+        nc.scalar.activation(tau[:], tz[:], ACT.Copy, scale=z_inv[:])
+        neg_z_inv = column("neg_z_inv")
+        nc.scalar.activation(neg_z_inv[:], z_inv[:], ACT.Copy, scale=-1.0)
+        neg_tau = column("neg_tau")
+        nc.scalar.activation(neg_tau[:], tz[:], ACT.Copy, scale=neg_z_inv[:])
+        neg_x2 = wide("neg_x2")
+        nc.scalar.activation(neg_x2[:], x[:], ACT.Identity, bias=tau[:], scale=-2.0)
+        pw = wide("pw")
+        nc.scalar.activation(pw[:], p, ACT.Square, scale=z_rsqrt[:])
+
+        big_f = wide("big_f")
+        nc.vector.scalar_tensor_tensor(big_f[:], c[:], GAIN, pw[:], ALU.mult, ALU.mult)
+        y = wide("y")
+        nc.vector.tensor_tensor(y[:], t_den[:], u[:], ALU.mult)
+        f = wide("f")
+        f_sum = column("f_sum")
+        nc.vector.scalar_tensor_tensor(f[:], big_f[:], 1.0, u[:], ALU.mult, ALU.mult, accum_out=f_sum[:])
+        neg_h = wide("neg_h")
+        nc.vector.tensor_tensor(neg_h[:], y[:], neg_x2[:], ALU.add)
+        e = wide("e")
+        nc.vector.tensor_tensor(e[:], f[:], u[:], ALU.mult)
+        neg_m = wide("neg_m")
+        nc.vector.tensor_tensor(neg_m[:], neg_h[:], y[:], ALU.add)
+        neg_tf = wide("neg_tf")
+        neg_tf_sum = column("neg_tf_sum")
+        nc.vector.scalar_tensor_tensor(neg_tf[:], f[:], 1.0, neg_h[:], ALU.mult, ALU.mult, accum_out=neg_tf_sum[:])
+
+        blocks = [slice(b * P, (b + 1) * P) for b in range(I // P)]
+        sums = [ps.tile([P, P], F32, name="sum%d" % b) for b in range(I // P)]
+
+        def add_turned(term, start=False, stop=False):
+            for b, cols in enumerate(blocks):
+                nc.tensor.matmul(sums[b][:], term[:, cols], ident[:], start=start, stop=stop, is_transpose=True)
+
+        share = column("share")
+        nc.scalar.activation(share[:], f_sum[:], ACT.Copy, scale=z_inv[:])
+        share_tp = wide("share_tp")
+        nc.scalar.activation(share_tp[:], tp_copy[:], ACT.Copy, scale=share[:])
+        add_turned(share_tp, start=True)
+        add_turned(neg_tf)
+        add_turned(neg_tf)
+        t_share = column("t_share")
+        nc.scalar.activation(t_share[:], neg_tf_sum[:], ACT.Copy, scale=neg_z_inv[:])
+        neg_beta = column("neg_beta")
+        nc.scalar.activation(neg_beta[:], share[:], ACT.Identity, bias=t_share[:], scale=neg_tau[:])
+        beta_p = wide("beta_p")
+        nc.scalar.activation(beta_p[:], p, ACT.Copy, scale=neg_beta[:])
+        add_turned(beta_p)
+
+        neg_em = wide("neg_em")
+        nc.vector.tensor_tensor(neg_em[:], e[:], neg_m[:], ALU.mult)
+        e_tp = wide("e_tp")
+        nc.vector.tensor_tensor(e_tp[:], e[:], tp_copy[:], ALU.mult)
+        w1 = wide("w1")
+        nc.vector.scalar_tensor_tensor(w1[:], neg_em[:], -1.0, p_rho[:], ALU.mult, ALU.mult)
+        rho_em = wide("rho_em")
+        nc.scalar.activation(rho_em[:], neg_em[:], ACT.Copy, scale=rho[:])
+        add_turned(rho_em)
+        w = wide("w")
+        nc.vector.tensor_tensor(w[:], w1[:], e_tp[:], ALU.add)
+        sent = wide("sent", 2 * I)
+        nc.vector.tensor_tensor(sent[:].indirect(links[:]), neg_tf[:], w[:], ALU.add)
+        add_turned(w, stop=True)
+        turned = [wide("turned%d" % b, P) for b in range(I // P)]
+        back = ps.tile([P, I], F32, name="back")
+        for b, cols in enumerate(blocks):
+            nc.scalar.copy(turned[b][:], sums[b][:])
+            nc.tensor.transpose(back[:, cols], turned[b][:], ident[:])
+        own = wide("own")
+        nc.scalar.activation(own[:], back[:], ACT.Copy, scale=-1.0)
+        nc.vector.tensor_tensor(placed[:].indirect(tokens[:]), own[:], sent[:, :I], ALU.add)
+
+        for n, (c0, c1) in enumerate(zip(OUT_EDGES, OUT_EDGES[1:])):
+            cols = slice(c0, c1)
+            result = wide("result%d" % n, c1 - c0)
+            nc.vector.tensor_tensor(result[:], placed[:, cols], base_sb[:, cols], ALU.add)
+            (nc.sync if n % 2 == 0 else nc.scalar).dma_start(out[:, cols], result[:])

@@ -18,7 +18,7 @@ PACK = 4
 T = 2048
 I = 512
 Q = 128
-SPARE = 64
+SPARE = 192
 GAIN = 512.0
 OUT_EDGES = (0, 640, 1280, 1792, 2048)
 FLOPS = 3 * 2 * 512 * Q * I
@@ -28,7 +28,6 @@ def tile_attend_hvneighbourshare_s_kernel(tc, query, keys_words, keys_scales, re
     nc = tc.nc
     with ExitStack() as ctx:
         sb = ctx.enter_context(tc.tile_pool(name="sb", bufs=1))
-        shared = ctx.enter_context(tc.tile_pool(name="shared", bufs=1))
         ps = ctx.enter_context(tc.psum_pool(name="ps", bufs=1))
 
         def wide(name, cols=I):
@@ -37,19 +36,20 @@ def tile_attend_hvneighbourshare_s_kernel(tc, query, keys_words, keys_scales, re
         def column(name):
             return sb.tile([P, 1], F32, name=name)
 
-        def load_scales(name, scales, clearer, tag):
-            plane = sb.tile([P, T], U8, name=name, tag=tag, align_bytes=64)
+        def load_scales(name, scales, clearer):
+            plane = sb.tile([P, T], U8, name=name)
             clearer.memset(plane[:].bitcast(I32), 0)
             for quad in range(4):
                 nc.sync.dma_start(plane[32 * quad : 32 * quad + 4, :].bitcast(I32), scales[0][4 * quad : 4 * quad + 4, :].bitcast(I32))
             return plane
 
-        def load_words(pool_words, words):
+        def load_words(name, words):
+            pool_words = sb.tile([P, T], I32, name=name)
             nc.sync.dma_start(pool_words[:], words[0].rearrange("p n t -> p (n t)").bitcast(I32))
             return pool_words
 
-        def load_rows(name, rows, offset):
-            raw = shared.tile([P, PACK, Q], F32, name=name, offset=offset)
+        def load_rows(name, rows):
+            raw = sb.tile([P, PACK, Q], F32, name=name)
             nc.sync.dma_start(raw[:], rows.rearrange("(p j) w -> p j w", j=PACK))
             return raw
 
@@ -76,14 +76,22 @@ def tile_attend_hvneighbourshare_s_kernel(tc, query, keys_words, keys_scales, re
 
         tokens = sb.tile([P, I // 16], U16, name="tokens")
         nc.sync.dma_start(tokens[:], offs)
-        q_raw = load_rows("q_raw", query, 4 * T)
+        q_raw = load_rows("q_raw", query)
         links = sb.tile([P, I // 16], U16, name="links")
         nc.sync.dma_start(links[:], offs2)
-        k_plane = load_scales("k_plane", keys_scales, nc.vector, "k_plane")
+        k_plane = load_scales("k_plane", keys_scales, nc.vector)
+        k_pool = load_words("k_pool", keys_words)
+        dq_raw = load_rows("dq_raw", dquery)
+        v_plane = load_scales("v_plane", vals_scales, nc.vector)
+        g_raw = load_rows("g_raw", gout)
+        rho = column("rho")
+        nc.sync.dma_start(rho[:], reserve)
+        v_pool = load_words("v_pool", vals_words)
+        base_sb = wide("base_sb", T)
+        nc.sync.dma_start(base_sb[:], base)
+
         ident = wide("ident", P)
         make_identity(nc, ident[:])
-        k_pool = load_words(shared.tile([P, T], I32, name="k_pool", offset=0), keys_words)
-
         p_win = wide("p_win", I + SPARE)
         tp_win = wide("tp_win", I + SPARE)
         nc.gpsimd.memset(p_win[:, I:], 0.0)
@@ -93,84 +101,55 @@ def tile_attend_hvneighbourshare_s_kernel(tc, query, keys_words, keys_scales, re
         p = p_win[:, :I]
         tp = tp_win[:, :I]
 
-        q_grouped = sb.tile([P, Q, PACK], BF16, name="q_grouped", tag="q_grouped", align_bytes=64)
+        q_grouped = sb.tile([P, Q, PACK], BF16, name="q_grouped", align_bytes=64)
         nc.vector.tensor_copy(q_grouped[:], q_raw[:].rearrange("p j w -> p w j"))
-        dq_raw = load_rows("dq_raw", dquery, 4 * T + 32)
-        rho = shared.tile([P, 1], F32, name="rho", offset=4 * T)
-        nc.sync.dma_start(rho[:], reserve)
         k_scales = gather_scales("k_scales", k_plane)
         q_mx = quantise("q", q_grouped)
-        v_plane = load_scales("v_plane", vals_scales, nc.gpsimd, "q_grouped")
         k_words = gather_words("k_words", k_pool)
-        v_pool = load_words(shared.tile([P, T], I32, name="v_pool", offset=0), vals_words)
         a = product("a", q_mx, k_words, k_scales)
 
         dq_grouped = sb.tile([P, Q, PACK], BF16, name="dq_grouped", align_bytes=64)
         nc.scalar.copy(dq_grouped[:], dq_raw[:].rearrange("p j w -> p w j"))
-        g_raw = load_rows("g_raw", gout, 4 * T + 32)
         dq_mx = quantise("dq", dq_grouped)
         x = product("x", dq_mx, k_words, k_scales)
         v_scales = gather_scales("v_scales", v_plane)
 
         z = column("z")
         nc.scalar.activation(p, a[:], ACT.Exp, accum_out=z[:])
-        p_rho = wide("p_rho")
-        nc.scalar.activation(p_rho[:], p, ACT.Identity, bias=rho[:])
         z_rsqrt = column("z_rsqrt")
         nc.scalar.activation(z_rsqrt[:], z[:], ACT.Abs_reciprocal_sqrt)
         z_inv = column("z_inv")
         nc.scalar.activation(z_inv[:], z_rsqrt[:], ACT.Square)
 
+        p2 = wide("p2")
+        nc.vector.tensor_copy(p2[:], p_win[:].indirect(links[:]))
+        den = wide("den")
+        nc.vector.scalar_tensor_tensor(den[:], p2[:], rho[:], p, ALU.add, ALU.add)
         tz = column("tz")
         nc.vector.scalar_tensor_tensor(tp, x[:], 1.0, p, ALU.mult, ALU.mult, accum_out=tz[:])
-        den = wide("den")
-        nc.vector.tensor_tensor(den[:], p_win[:].indirect(links[:]), p_rho[:], ALU.add)
-
-        tp_copy = wide("tp_copy")
-        nc.scalar.copy(tp_copy[:], tp)
         den_rsqrt = wide("den_rsqrt")
         nc.scalar.activation(den_rsqrt[:], den[:], ACT.Abs_reciprocal_sqrt)
         u = wide("u")
         nc.scalar.activation(u[:], den_rsqrt[:], ACT.Square)
 
-        t_den = wide("t_den")
-        nc.vector.tensor_tensor(t_den[:], tp_win[:].indirect(links[:]), tp_copy[:], ALU.add)
-
-        g_grouped = sb.tile([P, Q, PACK], BF16, name="g_grouped", align_bytes=64)
-        nc.scalar.copy(g_grouped[:], g_raw[:].rearrange("p j w -> p w j"))
+        tp2 = wide("tp2")
+        nc.vector.tensor_copy(tp2[:], tp_win[:].indirect(links[:]))
         v_words = gather_words("v_words", v_pool)
-        base_sb = shared.tile([P, T], F32, name="base_sb", offset=0)
-        nc.sync.dma_start(base_sb[:], base)
-        g_mx = quantise("g", g_grouped)
-        c = product("c", g_mx, v_words, v_scales)
+        t_den = wide("t_den")
+        nc.vector.tensor_tensor(t_den[:], tp2[:], tp, ALU.add)
 
-        tau = column("tau")
-        nc.scalar.activation(tau[:], tz[:], ACT.Copy, scale=z_inv[:])
         neg_z_inv = column("neg_z_inv")
         nc.scalar.activation(neg_z_inv[:], z_inv[:], ACT.Copy, scale=-1.0)
         neg_tau = column("neg_tau")
         nc.scalar.activation(neg_tau[:], tz[:], ACT.Copy, scale=neg_z_inv[:])
-        neg_x2 = wide("neg_x2")
-        nc.scalar.activation(neg_x2[:], x[:], ACT.Identity, bias=tau[:], scale=-2.0)
+        g_grouped = sb.tile([P, Q, PACK], BF16, name="g_grouped", align_bytes=64)
+        nc.scalar.copy(g_grouped[:], g_raw[:].rearrange("p j w -> p w j"))
+        g_mx = quantise("g", g_grouped)
+        c = product("c", g_mx, v_words, v_scales)
+        x2 = wide("x2")
+        nc.scalar.activation(x2[:], x[:], ACT.Identity, bias=neg_tau[:], scale=2.0)
         pw = wide("pw")
         nc.scalar.activation(pw[:], p, ACT.Square, scale=z_rsqrt[:])
-
-        big_f = wide("big_f")
-        nc.vector.scalar_tensor_tensor(big_f[:], c[:], GAIN, pw[:], ALU.mult, ALU.mult)
-        y = wide("y")
-        nc.vector.tensor_tensor(y[:], t_den[:], u[:], ALU.mult)
-        f = wide("f")
-        f_sum = column("f_sum")
-        nc.vector.scalar_tensor_tensor(f[:], big_f[:], 1.0, u[:], ALU.mult, ALU.mult, accum_out=f_sum[:])
-        neg_h = wide("neg_h")
-        nc.vector.tensor_tensor(neg_h[:], y[:], neg_x2[:], ALU.add)
-        e = wide("e")
-        nc.vector.tensor_tensor(e[:], f[:], u[:], ALU.mult)
-        neg_m = wide("neg_m")
-        nc.vector.tensor_tensor(neg_m[:], neg_h[:], y[:], ALU.add)
-        neg_tf = wide("neg_tf")
-        neg_tf_sum = column("neg_tf_sum")
-        nc.vector.scalar_tensor_tensor(neg_tf[:], f[:], 1.0, neg_h[:], ALU.mult, ALU.mult, accum_out=neg_tf_sum[:])
 
         blocks = [slice(b * P, (b + 1) * P) for b in range(I // P)]
         sums = [ps.tile([P, P], F32, name="sum%d" % b) for b in range(I // P)]
@@ -179,35 +158,57 @@ def tile_attend_hvneighbourshare_s_kernel(tc, query, keys_words, keys_scales, re
             for b, cols in enumerate(blocks):
                 nc.tensor.matmul(sums[b][:], term[:, cols], ident[:], start=start, stop=stop, is_transpose=True)
 
-        share = column("share")
-        nc.scalar.activation(share[:], f_sum[:], ACT.Copy, scale=z_inv[:])
-        share_tp = wide("share_tp")
-        nc.scalar.activation(share_tp[:], tp_copy[:], ACT.Copy, scale=share[:])
-        add_turned(share_tp, start=True)
-        add_turned(neg_tf)
-        add_turned(neg_tf)
-        t_share = column("t_share")
-        nc.scalar.activation(t_share[:], neg_tf_sum[:], ACT.Copy, scale=neg_z_inv[:])
-        neg_beta = column("neg_beta")
-        nc.scalar.activation(neg_beta[:], share[:], ACT.Identity, bias=t_share[:], scale=neg_tau[:])
-        beta_p = wide("beta_p")
-        nc.scalar.activation(beta_p[:], p, ACT.Copy, scale=neg_beta[:])
-        add_turned(beta_p)
+        y = wide("y")
+        nc.vector.tensor_tensor(y[:], t_den[:], u[:], ALU.mult)
+        big_f = wide("big_f")
+        nc.vector.scalar_tensor_tensor(big_f[:], c[:], GAIN, pw[:], ALU.mult, ALU.mult)
+        m = wide("m")
+        nc.vector.scalar_tensor_tensor(m[:], y[:], -2.0, x2[:], ALU.mult, ALU.add)
+        f = wide("f")
+        f_sum = column("f_sum")
+        nc.vector.scalar_tensor_tensor(f[:], big_f[:], 1.0, u[:], ALU.mult, ALU.mult, accum_out=f_sum[:])
+        e = wide("e")
+        nc.vector.tensor_tensor(e[:], f[:], u[:], ALU.mult)
 
-        neg_em = wide("neg_em")
-        nc.vector.tensor_tensor(neg_em[:], e[:], neg_m[:], ALU.mult)
-        e_tp = wide("e_tp")
-        nc.vector.tensor_tensor(e_tp[:], e[:], tp_copy[:], ALU.mult)
-        w1 = wide("w1")
-        nc.vector.scalar_tensor_tensor(w1[:], neg_em[:], -1.0, p_rho[:], ALU.mult, ALU.mult)
-        rho_em = wide("rho_em")
-        nc.scalar.activation(rho_em[:], neg_em[:], ACT.Copy, scale=rho[:])
-        add_turned(rho_em)
-        w = wide("w")
-        nc.vector.tensor_tensor(w[:], w1[:], e_tp[:], ALU.add)
+        neg_share = column("neg_share")
+        nc.scalar.activation(neg_share[:], f_sum[:], ACT.Copy, scale=neg_z_inv[:])
+        share_tp = wide("share_tp")
+        nc.scalar.activation(share_tp[:], tp, ACT.Copy, scale=neg_share[:])
+        add_turned(share_tp, start=True)
+        tau_share = column("tau_share")
+        nc.scalar.activation(tau_share[:], neg_share[:], ACT.Copy, scale=neg_tau[:])
+        rho_z = column("rho_z")
+        nc.scalar.activation(rho_z[:], rho[:], ACT.Copy, scale=z_inv[:])
+
+        em = wide("em")
+        em_sum = column("em_sum")
+        nc.vector.scalar_tensor_tensor(em[:], e[:], 1.0, m[:], ALU.mult, ALU.mult, accum_out=em_sum[:])
+        e_td = wide("e_td")
+        e_td_sum = column("e_td_sum")
+        nc.vector.scalar_tensor_tensor(e_td[:], e[:], 1.0, t_den[:], ALU.mult, ALU.mult, accum_out=e_td_sum[:])
+        add_turned(e_td)
+        d_em = wide("d_em")
+        d_em_sum = column("d_em_sum")
+        nc.vector.scalar_tensor_tensor(d_em[:], den[:], rho[:], em[:], ALU.add, ALU.mult, accum_out=d_em_sum[:])
+        add_turned(d_em)
+        beta0 = column("beta0")
+        nc.scalar.activation(beta0[:], em_sum[:], ACT.Identity, bias=tau_share[:], scale=rho_z[:])
+        beta1 = column("beta1")
+        nc.scalar.activation(beta1[:], e_td_sum[:], ACT.Identity, bias=beta0[:], scale=neg_z_inv[:])
+        beta = column("beta")
+        nc.scalar.activation(beta[:], d_em_sum[:], ACT.Identity, bias=beta1[:], scale=neg_z_inv[:])
+        beta_p = wide("beta_p")
+        nc.scalar.activation(beta_p[:], p, ACT.Copy, scale=beta[:])
+
+        b2 = wide("b2")
+        nc.vector.tensor_tensor(b2[:], e[:], tp2[:], ALU.mult)
+        add_turned(b2)
+        b1 = wide("b1")
+        nc.vector.tensor_tensor(b1[:], em[:], p2[:], ALU.mult)
         sent = wide("sent", 2 * I)
-        nc.vector.tensor_tensor(sent[:].indirect(links[:]), neg_tf[:], w[:], ALU.add)
-        add_turned(w, stop=True)
+        nc.vector.tensor_tensor(sent[:].indirect(links[:]), b1[:], b2[:], ALU.add)
+        add_turned(beta_p)
+        add_turned(b1, stop=True)
         turned = [wide("turned%d" % b, P) for b in range(I // P)]
         back = ps.tile([P, I], F32, name="back")
         for b, cols in enumerate(blocks):
@@ -220,5 +221,5 @@ def tile_attend_hvneighbourshare_s_kernel(tc, query, keys_words, keys_scales, re
         for n, (c0, c1) in enumerate(zip(OUT_EDGES, OUT_EDGES[1:])):
             cols = slice(c0, c1)
             result = wide("result%d" % n, c1 - c0)
-            nc.vector.tensor_tensor(result[:], placed[:, cols], base_sb[:, cols], ALU.add)
+            nc.vector.tensor_tensor(result[:], base_sb[:, cols], placed[:, cols], ALU.subtract)
             (nc.sync if n % 2 == 0 else nc.scalar).dma_start(out[:, cols], result[:])

@@ -20,7 +20,7 @@ I = 512
 Q = 128
 SPARE = 192
 GAIN = 512.0
-OUT_EDGES = (0, 640, 1280, 1792, 2048)
+OUT_EDGES = (0, 256, 768, 1280, 1792, 2048)
 FLOPS = 3 * 2 * 512 * Q * I
 
 
@@ -60,7 +60,7 @@ def tile_attend_hvneighbourshare_s_kernel(tc, query, keys_words, keys_scales, re
             return codes, scales
 
         def gather_words(name, pool_words):
-            picked = sb.tile([P, I], U32, name=name, align_bytes=64)
+            picked = sb.tile([P, I], U32, name=name, tag=name, align_bytes=64)
             nc.vector.tensor_copy(picked[:], pool_words[:].bitcast(U32).indirect(tokens[:]))
             return picked
 
@@ -70,10 +70,12 @@ def tile_attend_hvneighbourshare_s_kernel(tc, query, keys_words, keys_scales, re
             return picked
 
         def product(name, rows, words, scales):
-            bank = ps.tile([P, I], F32, name=name)
-            nc.tensor.matmul_mx(out=bank[:], lhsT=rows[0][:].bitcast(FP8X4), lhsT_scale=rows[1][:], rhs=words[:].bitcast(FP8X4), rhs_scale=scales[:], start=True, stop=True)
+            bank = ps.tile([P, words.shape[1]], F32, name=name, tag=name)
+            nc.tensor.matmul_mx(out=bank[:], lhsT=rows[0][:].bitcast(FP8X4), lhsT_scale=rows[1][:], rhs=words.bitcast(FP8X4), rhs_scale=scales, start=True, stop=True)
             return bank
 
+        halves = [slice(0, I // 2), slice(I // 2, I)]
+        entries = [slice(0, I // 32), slice(I // 32, I // 16)]
         tokens = sb.tile([P, I // 16], U16, name="tokens")
         nc.sync.dma_start(tokens[:], offs)
         q_raw = load_rows("q_raw", query)
@@ -96,8 +98,6 @@ def tile_attend_hvneighbourshare_s_kernel(tc, query, keys_words, keys_scales, re
         tp_win = wide("tp_win", I + SPARE)
         nc.gpsimd.memset(p_win[:, I:], 0.0)
         nc.gpsimd.memset(tp_win[:, I:], 0.0)
-        placed = wide("placed", T)
-        nc.gpsimd.memset(placed[:], 0.0)
         p = p_win[:, :I]
         tp = tp_win[:, :I]
 
@@ -105,19 +105,25 @@ def tile_attend_hvneighbourshare_s_kernel(tc, query, keys_words, keys_scales, re
         nc.vector.tensor_copy(q_grouped[:], q_raw[:].rearrange("p j w -> p w j"))
         k_scales = gather_scales("k_scales", k_plane)
         q_mx = quantise("q", q_grouped)
-        k_words = gather_words("k_words", k_pool)
-        a = product("a", q_mx, k_words, k_scales)
+        k_words = sb.tile([P, I], U32, name="k_words", align_bytes=64)
+        a = []
+        for h in range(2):
+            nc.vector.tensor_copy(k_words[:, halves[h]], k_pool[:].bitcast(U32).indirect(tokens[:, entries[h]]))
+            a.append(product("a%d" % h, q_mx, k_words[:, halves[h]], k_scales[:, halves[h]]))
 
         dq_grouped = sb.tile([P, Q, PACK], BF16, name="dq_grouped", align_bytes=64)
         nc.scalar.copy(dq_grouped[:], dq_raw[:].rearrange("p j w -> p w j"))
         dq_mx = quantise("dq", dq_grouped)
-        x = product("x", dq_mx, k_words, k_scales)
+        x = product("x", dq_mx, k_words[:], k_scales[:])
         v_scales = gather_scales("v_scales", v_plane)
 
-        z = column("z")
-        nc.scalar.activation(p, a[:], ACT.Exp, accum_out=z[:])
+        z = [column("z%d" % h) for h in range(2)]
+        for h in range(2):
+            nc.scalar.activation(p_win[:, halves[h]], a[h][:], ACT.Exp, accum_out=z[h][:])
+        g_grouped = sb.tile([P, Q, PACK], BF16, name="g_grouped", align_bytes=64)
+        nc.scalar.copy(g_grouped[:], g_raw[:].rearrange("p j w -> p w j"))
         z_rsqrt = column("z_rsqrt")
-        nc.scalar.activation(z_rsqrt[:], z[:], ACT.Abs_reciprocal_sqrt)
+        nc.scalar.activation(z_rsqrt[:], z[0][:], ACT.Abs_reciprocal_sqrt, bias=z[1][:])
         z_inv = column("z_inv")
         nc.scalar.activation(z_inv[:], z_rsqrt[:], ACT.Square)
 
@@ -132,43 +138,46 @@ def tile_attend_hvneighbourshare_s_kernel(tc, query, keys_words, keys_scales, re
         u = wide("u")
         nc.scalar.activation(u[:], den_rsqrt[:], ACT.Square)
 
+        g_mx = quantise("g", g_grouped)
         tp2 = wide("tp2")
         nc.vector.tensor_copy(tp2[:], tp_win[:].indirect(links[:]))
+        r = wide("r")
+        nc.vector.tensor_tensor(r[:], p, u[:], ALU.mult)
+        r_sq = wide("r_sq")
+        nc.scalar.activation(r_sq[:], r[:], ACT.Square)
+        gain_z = column("gain_z")
+        nc.scalar.activation(gain_z[:], z_inv[:], ACT.Copy, scale=GAIN)
         v_words = gather_words("v_words", v_pool)
         t_den = wide("t_den")
-        nc.vector.tensor_tensor(t_den[:], tp2[:], tp, ALU.add)
+        nc.gpsimd.tensor_tensor(t_den[:], tp2[:], tp, ALU.add)
 
         neg_z_inv = column("neg_z_inv")
         nc.scalar.activation(neg_z_inv[:], z_inv[:], ACT.Copy, scale=-1.0)
         neg_tau = column("neg_tau")
         nc.scalar.activation(neg_tau[:], tz[:], ACT.Copy, scale=neg_z_inv[:])
-        g_grouped = sb.tile([P, Q, PACK], BF16, name="g_grouped", align_bytes=64)
-        nc.scalar.copy(g_grouped[:], g_raw[:].rearrange("p j w -> p w j"))
-        g_mx = quantise("g", g_grouped)
-        c = product("c", g_mx, v_words, v_scales)
+        c = product("c", g_mx, v_words[:], v_scales[:])
+        placed = sb.tile([P, T], F32, name="placed", tag="v_words", align_bytes=64)
+        nc.gpsimd.memset(placed[:], 0.0)
         x2 = wide("x2")
         nc.scalar.activation(x2[:], x[:], ACT.Identity, bias=neg_tau[:], scale=2.0)
-        pw = wide("pw")
-        nc.scalar.activation(pw[:], p, ACT.Square, scale=z_rsqrt[:])
 
         blocks = [slice(b * P, (b + 1) * P) for b in range(I // P)]
         sums = [ps.tile([P, P], F32, name="sum%d" % b) for b in range(I // P)]
 
-        def add_turned(term, start=False, stop=False):
-            for b, cols in enumerate(blocks):
+        def add_turned(term, start=False, stop=False, which=range(I // P)):
+            for b in which:
+                cols = blocks[b]
                 nc.tensor.matmul(sums[b][:], term[:, cols], ident[:], start=start, stop=stop, is_transpose=True)
 
         y = wide("y")
         nc.vector.tensor_tensor(y[:], t_den[:], u[:], ALU.mult)
-        big_f = wide("big_f")
-        nc.vector.scalar_tensor_tensor(big_f[:], c[:], GAIN, pw[:], ALU.mult, ALU.mult)
+        e = wide("e")
+        nc.vector.scalar_tensor_tensor(e[:], c[:], gain_z[:], r_sq[:], ALU.mult, ALU.mult)
         m = wide("m")
         nc.vector.scalar_tensor_tensor(m[:], y[:], -2.0, x2[:], ALU.mult, ALU.add)
         f = wide("f")
         f_sum = column("f_sum")
-        nc.vector.scalar_tensor_tensor(f[:], big_f[:], 1.0, u[:], ALU.mult, ALU.mult, accum_out=f_sum[:])
-        e = wide("e")
-        nc.vector.tensor_tensor(e[:], f[:], u[:], ALU.mult)
+        nc.vector.scalar_tensor_tensor(f[:], e[:], 1.0, den[:], ALU.mult, ALU.mult, accum_out=f_sum[:])
 
         neg_share = column("neg_share")
         nc.scalar.activation(neg_share[:], f_sum[:], ACT.Copy, scale=neg_z_inv[:])
@@ -203,20 +212,23 @@ def tile_attend_hvneighbourshare_s_kernel(tc, query, keys_words, keys_scales, re
         b2 = wide("b2")
         nc.vector.tensor_tensor(b2[:], e[:], tp2[:], ALU.mult)
         add_turned(b2)
-        b1 = wide("b1")
-        nc.vector.tensor_tensor(b1[:], em[:], p2[:], ALU.mult)
-        sent = wide("sent", 2 * I)
-        nc.vector.tensor_tensor(sent[:].indirect(links[:]), b1[:], b2[:], ALU.add)
         add_turned(beta_p)
-        add_turned(b1, stop=True)
-        turned = [wide("turned%d" % b, P) for b in range(I // P)]
-        back = ps.tile([P, I], F32, name="back")
-        for b, cols in enumerate(blocks):
-            nc.scalar.copy(turned[b][:], sums[b][:])
-            nc.tensor.transpose(back[:, cols], turned[b][:], ident[:])
+        b1 = wide("b1")
+        sent = wide("sent")
+        for h in range(2):
+            nc.vector.tensor_tensor(b1[:, halves[h]], em[:, halves[h]], p2[:, halves[h]], ALU.mult)
+            add_turned(b1, stop=True, which=(2 * h, 2 * h + 1))
+        for h in range(2):
+            nc.vector.tensor_tensor(sent[:].indirect(links[:, entries[h]]), b1[:, halves[h]], b2[:, halves[h]], ALU.add)
         own = wide("own")
-        nc.scalar.activation(own[:], back[:], ACT.Copy, scale=-1.0)
-        nc.vector.tensor_tensor(placed[:].indirect(tokens[:]), own[:], sent[:, :I], ALU.add)
+        for h, spent in enumerate(("a0", "a1")):
+            back = ps.tile([P, I // 2], F32, name="back%d" % h, tag=spent)
+            for j in range(2):
+                turned = wide("turned%d" % (2 * h + j), P)
+                nc.scalar.copy(turned[:], sums[2 * h + j][:])
+                nc.tensor.transpose(back[:, blocks[j]], turned[:], ident[:])
+            nc.scalar.activation(own[:, halves[h]], back[:], ACT.Copy, scale=-1.0)
+        nc.vector.tensor_tensor(placed[:].indirect(tokens[:]), own[:], sent[:], ALU.add)
 
         for n, (c0, c1) in enumerate(zip(OUT_EDGES, OUT_EDGES[1:])):
             cols = slice(c0, c1)

from contextlib import ExitStack

import concourse.mybir as mybir
from concourse.masks import make_identity

F32 = mybir.dt.float32
BF16 = mybir.dt.bfloat16
I32 = mybir.dt.int32
U32 = mybir.dt.uint32
U16 = mybir.dt.uint16
U8 = mybir.dt.uint8
FP8X4 = mybir.dt.float8_e4m3fn_x4
ACT = mybir.ActivationFunctionType
ALU = mybir.AluOpType

P = 128
PACK = 4
T = 2048
I = 512
Q = 128
SPARE = 192
GAIN = 512.0
OUT_EDGES = (0, 256, 768, 1280, 1792, 2048)
FLOPS = 3 * 2 * 512 * Q * I


def tile_attend_hvneighbourshare_s_kernel(tc, query, keys_words, keys_scales, reserve, gout, vals_words, vals_scales, dquery, base, offs2, offs, out):
    nc = tc.nc
    with ExitStack() as ctx:
        sb = ctx.enter_context(tc.tile_pool(name="sb", bufs=1))
        ps = ctx.enter_context(tc.psum_pool(name="ps", bufs=1))

        def wide(name, cols=I):
            return sb.tile([P, cols], F32, name=name)

        def column(name):
            return sb.tile([P, 1], F32, name=name)

        def load_scales(name, scales, clearer):
            plane = sb.tile([P, T], U8, name=name)
            clearer.memset(plane[:].bitcast(I32), 0)
            for quad in range(4):
                nc.sync.dma_start(plane[32 * quad : 32 * quad + 4, :].bitcast(I32), scales[0][4 * quad : 4 * quad + 4, :].bitcast(I32))
            return plane

        def load_words(name, words):
            pool_words = sb.tile([P, T], I32, name=name)
            nc.sync.dma_start(pool_words[:], words[0].rearrange("p n t -> p (n t)").bitcast(I32))
            return pool_words

        def load_rows(name, rows):
            raw = sb.tile([P, PACK, Q], F32, name=name)
            nc.sync.dma_start(raw[:], rows.rearrange("(p j) w -> p j w", j=PACK))
            return raw

        def quantise(name, grouped):
            codes = sb.tile([P, Q], U32, name=name + "_codes", align_bytes=64)
            scales = sb.tile([P, Q], U8, name=name + "_scales", align_bytes=64)
            nc.vector.quantize_mx(out=codes[:].bitcast(FP8X4), scales=scales[:], in_=grouped[:].rearrange("p w j -> p (w j)"))
            return codes, scales

        def gather_words(name, pool_words):
            picked = sb.tile([P, I], U32, name=name, tag=name, align_bytes=64)
            nc.vector.tensor_copy(picked[:], pool_words[:].bitcast(U32).indirect(tokens[:]))
            return picked

        def gather_scales(name, plane):
            picked = sb.tile([P, I], U8, name=name, align_bytes=64)
            nc.vector.tensor_copy(picked[:], plane[:].indirect(tokens[:]))
            return picked

        def product(name, rows, words, scales):
            bank = ps.tile([P, words.shape[1]], F32, name=name, tag=name)
            nc.tensor.matmul_mx(out=bank[:], lhsT=rows[0][:].bitcast(FP8X4), lhsT_scale=rows[1][:], rhs=words.bitcast(FP8X4), rhs_scale=scales, start=True, stop=True)
            return bank

        halves = [slice(0, I // 2), slice(I // 2, I)]
        entries = [slice(0, I // 32), slice(I // 32, I // 16)]
        tokens = sb.tile([P, I // 16], U16, name="tokens")
        nc.sync.dma_start(tokens[:], offs)
        q_raw = load_rows("q_raw", query)
        links = sb.tile([P, I // 16], U16, name="links")
        nc.sync.dma_start(links[:], offs2)
        k_plane = load_scales("k_plane", keys_scales, nc.vector)
        k_pool = load_words("k_pool", keys_words)
        dq_raw = load_rows("dq_raw", dquery)
        v_plane = load_scales("v_plane", vals_scales, nc.vector)
        g_raw = load_rows("g_raw", gout)
        rho = column("rho")
        nc.sync.dma_start(rho[:], reserve)
        v_pool = load_words("v_pool", vals_words)
        base_sb = wide("base_sb", T)
        nc.sync.dma_start(base_sb[:], base)

        ident = wide("ident", P)
        make_identity(nc, ident[:])
        p_win = wide("p_win", I + SPARE)
        tp_win = wide("tp_win", I + SPARE)
        nc.gpsimd.memset(p_win[:, I:], 0.0)
        nc.gpsimd.memset(tp_win[:, I:], 0.0)
        p = p_win[:, :I]
        tp = tp_win[:, :I]

        q_grouped = sb.tile([P, Q, PACK], BF16, name="q_grouped", align_bytes=64)
        nc.vector.tensor_copy(q_grouped[:], q_raw[:].rearrange("p j w -> p w j"))
        k_scales = gather_scales("k_scales", k_plane)
        q_mx = quantise("q", q_grouped)
        k_words = sb.tile([P, I], U32, name="k_words", align_bytes=64)
        a = []
        for h in range(2):
            nc.vector.tensor_copy(k_words[:, halves[h]], k_pool[:].bitcast(U32).indirect(tokens[:, entries[h]]))
            a.append(product("a%d" % h, q_mx, k_words[:, halves[h]], k_scales[:, halves[h]]))

        dq_grouped = sb.tile([P, Q, PACK], BF16, name="dq_grouped", align_bytes=64)
        nc.scalar.copy(dq_grouped[:], dq_raw[:].rearrange("p j w -> p w j"))
        dq_mx = quantise("dq", dq_grouped)
        x = product("x", dq_mx, k_words[:], k_scales[:])
        v_scales = gather_scales("v_scales", v_plane)

        z = [column("z%d" % h) for h in range(2)]
        for h in range(2):
            nc.scalar.activation(p_win[:, halves[h]], a[h][:], ACT.Exp, accum_out=z[h][:])
        g_grouped = sb.tile([P, Q, PACK], BF16, name="g_grouped", align_bytes=64)
        nc.scalar.copy(g_grouped[:], g_raw[:].rearrange("p j w -> p w j"))
        z_rsqrt = column("z_rsqrt")
        nc.scalar.activation(z_rsqrt[:], z[0][:], ACT.Abs_reciprocal_sqrt, bias=z[1][:])
        z_inv = column("z_inv")
        nc.scalar.activation(z_inv[:], z_rsqrt[:], ACT.Square)

        p2 = wide("p2")
        nc.vector.tensor_copy(p2[:], p_win[:].indirect(links[:]))
        den = wide("den")
        nc.vector.scalar_tensor_tensor(den[:], p2[:], rho[:], p, ALU.add, ALU.add)
        tz = column("tz")
        nc.vector.scalar_tensor_tensor(tp, x[:], 1.0, p, ALU.mult, ALU.mult, accum_out=tz[:])
        den_rsqrt = wide("den_rsqrt")
        nc.scalar.activation(den_rsqrt[:], den[:], ACT.Abs_reciprocal_sqrt)
        u = wide("u")
        nc.scalar.activation(u[:], den_rsqrt[:], ACT.Square)

        g_mx = quantise("g", g_grouped)
        tp2 = wide("tp2")
        nc.vector.tensor_copy(tp2[:], tp_win[:].indirect(links[:]))
        r = wide("r")
        nc.vector.tensor_tensor(r[:], p, u[:], ALU.mult)
        r_sq = wide("r_sq")
        nc.scalar.activation(r_sq[:], r[:], ACT.Square)
        gain_z = column("gain_z")
        nc.scalar.activation(gain_z[:], z_inv[:], ACT.Copy, scale=GAIN)
        v_words = gather_words("v_words", v_pool)
        t_den = wide("t_den")
        nc.gpsimd.tensor_tensor(t_den[:], tp2[:], tp, ALU.add)

        neg_z_inv = column("neg_z_inv")
        nc.scalar.activation(neg_z_inv[:], z_inv[:], ACT.Copy, scale=-1.0)
        neg_tau = column("neg_tau")
        nc.scalar.activation(neg_tau[:], tz[:], ACT.Copy, scale=neg_z_inv[:])
        c = product("c", g_mx, v_words[:], v_scales[:])
        placed = sb.tile([P, T], F32, name="placed", tag="v_words", align_bytes=64)
        nc.gpsimd.memset(placed[:], 0.0)
        x2 = wide("x2")
        nc.scalar.activation(x2[:], x[:], ACT.Identity, bias=neg_tau[:], scale=2.0)

        blocks = [slice(b * P, (b + 1) * P) for b in range(I // P)]
        sums = [ps.tile([P, P], F32, name="sum%d" % b) for b in range(I // P)]

        def add_turned(term, start=False, stop=False, which=range(I // P)):
            for b in which:
                cols = blocks[b]
                nc.tensor.matmul(sums[b][:], term[:, cols], ident[:], start=start, stop=stop, is_transpose=True)

        y = wide("y")
        nc.vector.tensor_tensor(y[:], t_den[:], u[:], ALU.mult)
        e = wide("e")
        nc.vector.scalar_tensor_tensor(e[:], c[:], gain_z[:], r_sq[:], ALU.mult, ALU.mult)
        m = wide("m")
        nc.vector.scalar_tensor_tensor(m[:], y[:], -2.0, x2[:], ALU.mult, ALU.add)
        f = wide("f")
        f_sum = column("f_sum")
        nc.vector.scalar_tensor_tensor(f[:], e[:], 1.0, den[:], ALU.mult, ALU.mult, accum_out=f_sum[:])

        neg_share = column("neg_share")
        nc.scalar.activation(neg_share[:], f_sum[:], ACT.Copy, scale=neg_z_inv[:])
        share_tp = wide("share_tp")
        nc.scalar.activation(share_tp[:], tp, ACT.Copy, scale=neg_share[:])
        add_turned(share_tp, start=True)
        tau_share = column("tau_share")
        nc.scalar.activation(tau_share[:], neg_share[:], ACT.Copy, scale=neg_tau[:])
        rho_z = column("rho_z")
        nc.scalar.activation(rho_z[:], rho[:], ACT.Copy, scale=z_inv[:])

        em = wide("em")
        em_sum = column("em_sum")
        nc.vector.scalar_tensor_tensor(em[:], e[:], 1.0, m[:], ALU.mult, ALU.mult, accum_out=em_sum[:])
        e_td = wide("e_td")
        e_td_sum = column("e_td_sum")
        nc.vector.scalar_tensor_tensor(e_td[:], e[:], 1.0, t_den[:], ALU.mult, ALU.mult, accum_out=e_td_sum[:])
        add_turned(e_td)
        d_em = wide("d_em")
        d_em_sum = column("d_em_sum")
        nc.vector.scalar_tensor_tensor(d_em[:], den[:], rho[:], em[:], ALU.add, ALU.mult, accum_out=d_em_sum[:])
        add_turned(d_em)
        beta0 = column("beta0")
        nc.scalar.activation(beta0[:], em_sum[:], ACT.Identity, bias=tau_share[:], scale=rho_z[:])
        beta1 = column("beta1")
        nc.scalar.activation(beta1[:], e_td_sum[:], ACT.Identity, bias=beta0[:], scale=neg_z_inv[:])
        beta = column("beta")
        nc.scalar.activation(beta[:], d_em_sum[:], ACT.Identity, bias=beta1[:], scale=neg_z_inv[:])
        beta_p = wide("beta_p")
        nc.scalar.activation(beta_p[:], p, ACT.Copy, scale=beta[:])

        b2 = wide("b2")
        nc.vector.tensor_tensor(b2[:], e[:], tp2[:], ALU.mult)
        add_turned(b2)
        add_turned(beta_p)
        b1 = wide("b1")
        sent = wide("sent")
        for h in range(2):
            nc.vector.tensor_tensor(b1[:, halves[h]], em[:, halves[h]], p2[:, halves[h]], ALU.mult)
            add_turned(b1, stop=True, which=(2 * h, 2 * h + 1))
        for h in range(2):
            nc.vector.tensor_tensor(sent[:].indirect(links[:, entries[h]]), b1[:, halves[h]], b2[:, halves[h]], ALU.add)
        own = wide("own")
        for h, spent in enumerate(("a0", "a1")):
            back = ps.tile([P, I // 2], F32, name="back%d" % h, tag=spent)
            for j in range(2):
                turned = wide("turned%d" % (2 * h + j), P)
                nc.scalar.copy(turned[:], sums[2 * h + j][:])
                nc.tensor.transpose(back[:, blocks[j]], turned[:], ident[:])
            nc.scalar.activation(own[:, halves[h]], back[:], ACT.Copy, scale=-1.0)
        nc.vector.tensor_tensor(placed[:].indirect(tokens[:]), own[:], sent[:], ALU.add)

        for n, (c0, c1) in enumerate(zip(OUT_EDGES, OUT_EDGES[1:])):
            cols = slice(c0, c1)
            result = wide("result%d" % n, c1 - c0)
            nc.vector.tensor_tensor(result[:], base_sb[:, cols], placed[:, cols], ALU.subtract)
            (nc.sync if n % 2 == 0 else nc.scalar).dma_start(out[:, cols], result[:])
